import numpy as np
import ml_dtypes


def mxq(x, axis, fmt="e4m3"):
    dtype, down = {"e4m3": (ml_dtypes.float8_e4m3fn, 7), "e5m2": (ml_dtypes.float8_e5m2, 14)}[fmt]
    v = np.moveaxis(np.asarray(x, np.float32).astype(ml_dtypes.bfloat16).astype(np.float64), axis, -1)
    blocks = v.reshape(v.shape[:-1] + (-1, 32))
    amax = np.abs(blocks).max(-1, keepdims=True)
    byte = np.maximum(np.where(amax > 0, np.frexp(amax)[1] - 1 + 127, 0) - down, 1)
    scale = np.exp2(byte - 127.0)
    codes = (blocks / scale).astype(np.float32).astype(dtype).astype(np.float64)
    return np.moveaxis((codes * scale).reshape(v.shape), -1, axis)


WIDE = False


def mx_kscale(k):
    if not WIDE:
        return np.ones(k)
    levels = np.array([10, -10, 5, -5, 0])
    if k % 512:
        return np.exp2(np.random.permutation(np.resize(levels, k // 32))).repeat(32)
    a = np.empty((k // 512, 16))
    for p in range(k // 512):
        a[p, :8] = np.random.permutation(np.resize(levels, 8))
        for g in range(8):
            far = levels[np.abs(levels - a[p, g]) >= 10]
            a[p, g + 8] = far[np.random.randint(len(far))]
    return np.exp2(a.ravel()).repeat(32)


def f64(x):
    return np.asarray(x).astype(np.float64)


def striped(idx):
    return np.tile(idx.reshape(-1, 16).T, (8, 1)).astype(np.uint16)


def unstriped(offs):
    return offs[:16].T.reshape(-1).astype(np.int64)


E2M1 = np.array([0.0, 0.5, 1.0, 1.5, 2.0, 3.0, 4.0, 6.0, -0.0, -0.5, -1.0, -1.5, -2.0, -3.0, -4.0, -6.0])


def pack_weight(w, fmt):
    k, n = w.shape
    w = f64(np.asarray(w, np.float32).astype(ml_dtypes.bfloat16)).reshape(k // 32, 32, n)
    amax = np.abs(w).max(1)
    if fmt == "e4m3":
        byte = np.frexp(amax)[1] - 1 + 127 - 7
    else:
        mant, ex = np.frexp(amax / 6.0)
        byte = np.where(mant > 0.5, ex, ex - 1) + 127
    byte = np.clip(np.where(amax > 0, byte, 1), 1, 254)
    scaled = (w * np.exp2(127.0 - byte)[:, None, :]).reshape(k, n).astype(np.float32)
    by_word = np.ascontiguousarray(scaled.reshape(k // 512, 128, 4, n).transpose(0, 1, 3, 2))
    if fmt == "e4m3":
        words = by_word.astype(ml_dtypes.float8_e4m3fn).view(np.uint8)
    else:
        c = by_word.astype(ml_dtypes.float4_e2m1fn).view(np.uint8) & 0xF
        words = (c[..., 0::2] | (c[..., 1::2] << 4)).reshape(k // 512, 128, 2 * n)
    return np.ascontiguousarray(words), np.ascontiguousarray(byte.astype(np.uint8).reshape(k // 512, 16, n))


def unpack_weight(words, scales, fmt):
    g, _, n = scales.shape
    words = np.ascontiguousarray(words).reshape(g, 128, n, -1)
    if fmt == "e4m3":
        vals = words.view(ml_dtypes.float8_e4m3fn).astype(np.float64)
    else:
        nib = np.empty((g, 128, n, 4), np.uint8)
        nib[..., 0::2] = words & 0xF
        nib[..., 1::2] = words >> 4
        vals = E2M1[nib]
    vals = vals * np.repeat(np.exp2(scales.astype(np.float64) - 127.0), 8, axis=1)[..., None]
    return vals.transpose(0, 1, 3, 2).reshape(g * 512, n)


def gelu(v):
    return 0.5 * v * (1.0 + np.tanh(np.sqrt(2.0 / np.pi) * (v + 0.044715 * v**3)))


K, H, T, S, P = 512, 1024, 4096, 1024, 512

def setup_inputs():
    n = np.random.standard_normal
    s = mx_kscale(K)[:, None]
    u = mx_kscale(H)[:, None]
    tab_words, tab_scales = pack_weight(n((K, T)) * s, "e4m3")
    w2_words, w2_scales = pack_weight(n((K, H)) / np.sqrt(K) / s, "e2m1")
    w3_words, w3_scales = pack_weight(n((K, H)) / np.sqrt(K) / s, "e4m3")
    return {
        "tab_words": tab_words, "tab_scales": tab_scales,
        "offs": striped(np.random.permutation(T)[:S]),
        "pos1": striped(np.random.permutation(S)[:P]),
        "w1": (n((K, H)) / np.sqrt(K) / s).astype(np.float32),
        "w2_words": w2_words, "w2_scales": w2_scales,
        "w3_words": w3_words, "w3_scales": w3_scales,
        "gain": (np.exp(0.3 * n(H)) * u[:, 0]).astype(np.float32),
        "w4": (1.3 * n((H, H)) / np.sqrt(H) / u).astype(np.float32),
        "ribbon": n((H, P)).astype(np.float32),
        "skip": (0.7 * np.exp(0.3 * n(H)) / u[:, 0]).astype(np.float32),
        "wgo": np.exp(0.3 * n((128, P))).astype(np.float32),
    }

def reference(tab_words, tab_scales, offs, pos1, w1, w2_words, w2_scales, w3_words, w3_scales, gain, w4, ribbon, skip, wgo):
    v = unpack_weight(tab_words, tab_scales, "e4m3")[:, unstriped(offs)]
    b1 = mxq(f64(w1), 0, "e4m3").T @ v
    b2 = unpack_weight(w2_words, w2_scales, "e2m1").T @ v
    b3 = unpack_weight(w3_words, w3_scales, "e4m3").T @ v
    h = f64(gain)[:, None] * np.maximum(np.maximum(b1, b2), b3)
    out = f64(skip)[:, None] * h
    x = mxq(h[:, unstriped(pos1)], 0, "e4m3")
    d = mxq(f64(w4), 0, "e4m3").T @ x
    y = np.tanh(d) * f64(ribbon) + out[:, unstriped(pos1)]
    out[:, unstriped(pos1)] = np.tile(f64(wgo), (H // 128, 1)) * y
    return out

@@ -1,0 +1,276 @@
+from contextlib import ExitStack
+
+import concourse.mybir as mybir
+
+K, H, T, S, PICK = 512, 1024, 4096, 1024, 512
+FLOPS = 3 * 2 * K * H * S + 2 * H * H * PICK
+
+F32 = mybir.dt.float32
+BF16 = mybir.dt.bfloat16
+I32 = mybir.dt.int32
+U32 = mybir.dt.uint32
+U16 = mybir.dt.uint16
+U8 = mybir.dt.uint8
+FP8X4 = mybir.dt.float8_e4m3fn_x4
+FP4X4 = mybir.dt.float4_e2m1fn_x4
+ALU = mybir.AluOpType
+ACT = mybir.ActivationFunctionType
+
+P = 128
+PACK = 4
+KP = P * PACK
+NB = H // KP
+NT = NB * PACK
+BANK = 512
+W3_ROW = 4
+
+
+def tile_list_printhead_dot_features_kernel(
+    tc, tab_words, tab_scales, offs, pos1, w1, w2_words, w2_scales, w3_words, w3_scales, gain, w4, ribbon, skip, wgo, out
+):
+    nc = tc.nc
+    with ExitStack() as ctx:
+        lists = ctx.enter_context(tc.tile_pool(name="lists", bufs=1))
+        keep = ctx.enter_context(tc.tile_pool(name="keep", bufs=1))
+        ring = ctx.enter_context(tc.tile_pool(name="ring", bufs=3))
+        psum = ctx.enter_context(tc.psum_pool(name="psum", bufs=8))
+
+        idx = lists.tile([P, S // 16], U16, name="idx")
+        nc.sync.dma_start(idx[:], offs)
+        p1 = lists.tile([P, PICK // 16], U16, name="p1")
+        nc.sync.dma_start(p1[:], pos1)
+
+        def load_weight(src_rows, b, stage):
+            raw = keep.tile([P, PACK, KP], F32, name="raw", tag=stage)
+            nc.sync.dma_start(raw[:], src_rows[:, b * KP:(b + 1) * KP].rearrange("(p j) c -> p j c", j=PACK))
+            return raw
+
+        def round_weight(raw, pieces):
+            grouped = ring.tile([P, PACK * KP], BF16, name="grouped", tag="grouped", bufs=3, align_bytes=64)
+            dst = grouped[:].rearrange("p (t m j) -> p m t j", t=PACK, j=PACK)
+            src = raw[:].rearrange("p j (m t) -> p m t j", t=PACK)
+            step = P // pieces
+            for s in range(pieces):
+                nc.scalar.copy(out=dst[:, s * step:(s + 1) * step], in_=src[:, s * step:(s + 1) * step])
+            return grouped
+
+        def mx_tiles(name):
+            codes = keep.tile([P, KP], U32, name=name + "_codes", align_bytes=64)
+            scales = keep.tile([P, KP], U8, name=name + "_scales", align_bytes=64)
+            return codes, scales
+
+        def quantise_cols(tiles, grouped, c0, c1):
+            nc.vector.quantize_mx(out=tiles[0][:, c0:c1].bitcast(FP8X4), scales=tiles[1][:, c0:c1], in_=grouped[:, PACK * c0:PACK * c1])
+
+        def quantise(grouped, name):
+            tiles = mx_tiles(name)
+            quantise_cols(tiles, grouped, 0, KP)
+            return tiles
+
+        gain_sb = keep.tile([P, NT], F32, name="gain_sb")
+        nc.sync.dma_start(gain_sb[:].rearrange("p (b i) -> p b i", i=PACK), gain.rearrange("(b p i) -> p b i", b=NB, i=PACK))
+        skip_sb = keep.tile([P, NT], F32, name="skip_sb")
+        nc.sync.dma_start(skip_sb[:].rearrange("p (b i) -> p b i", i=PACK), skip.rearrange("(b p i) -> p b i", b=NB, i=PACK))
+        w1_raw = load_weight(w1, 0, "stage_a")
+        w2_dram = w2_words[0].bitcast(I32)
+        w3_dram = w3_words[0].rearrange("p n t -> p (n t)").bitcast(I32)
+
+        def load_packed(b):
+            w2_raw = keep.tile([P, 2 * KP], U8, name="w2_raw", tag="stage_c")
+            nc.sync.dma_start(w2_raw[:].bitcast(I32), w2_dram[:, b * KP // 2:(b + 1) * KP // 2])
+            w3_raw = keep.tile([P, KP], U32, name="w3_raw", tag="stage_d")
+            nc.sync.dma_start(w3_raw[:].bitcast(I32), w3_dram[:, b * KP:(b + 1) * KP])
+            return w2_raw, w3_raw
+
+        w23_raw = load_packed(0)
+        gs = keep.tile([P, NT], F32, name="gs")
+        nc.vector.tensor_tensor(gs[:], gain_sb[:], skip_sb[:], ALU.mult)
+        tab_w = keep.tile([P, T], U32, name="tab_w", tag="big")
+        nc.sync.dma_start(tab_w[:].bitcast(I32), tab_words[0].rearrange("p n t -> p (n t)").bitcast(I32))
+        tab_s = keep.tile([P, T], U8, name="tab_s", tag="stage_b")
+        nc.vector.memset(tab_s[:].bitcast(I32), 0)
+        for q in range(4):
+            nc.scalar.dma_start(tab_s[32 * q:32 * q + 4, :].bitcast(I32), tab_scales[0, 4 * q:4 * q + 4, :].bitcast(I32))
+        ws_raw = keep.tile([P, H], U8, name="ws_raw")
+        nc.gpsimd.memset(ws_raw[:].bitcast(I32), 0)
+        for q in range(4):
+            r0 = 32 * q + W3_ROW
+            nc.gpsimd.dma_start(ws_raw[r0:r0 + 4, :].bitcast(I32), w3_scales[0, 4 * q:4 * q + 4, :].bitcast(I32))
+        for q in range(4):
+            queue = nc.gpsimd if q == 0 else nc.sync
+            queue.dma_start(ws_raw[32 * q:32 * q + 4, :].bitcast(I32), w2_scales[0, 4 * q:4 * q + 4, :].bitcast(I32))
+
+        w1_grouped = round_weight(w1_raw, 1)
+        v_s = keep.tile([P, S], U8, name="v_s", align_bytes=64)
+        nc.vector.tensor_copy(v_s[:], tab_s[:].indirect(idx[:]))
+        w1q = {0: quantise(w1_grouped, "w1q0")}
+        v_w = []
+        for hf in range(S // BANK):
+            vw = keep.tile([P, BANK], U32, name="v_w%d" % hf, align_bytes=64)
+            cols = BANK // 16
+            nc.vector.tensor_copy(vw[:], tab_w[:].indirect(idx[:, hf * cols:(hf + 1) * cols]))
+            v_w.append(vw)
+
+        def deal_packed(b, w2_raw, w3_raw):
+            w3c = keep.tile([P, KP], U32, name="w3c%d" % b, align_bytes=64)
+            nc.scalar.copy(out=w3c[:].rearrange("p (i m) -> p m i", i=PACK), in_=w3_raw[:].rearrange("p (m i) -> p m i", i=PACK))
+            w2c = keep.tile([P, 2 * KP], U8, name="w2c%d" % b, align_bytes=64)
+            nc.scalar.copy(
+                out=w2c[:].bitcast(U16).rearrange("p (i m) -> p m i", i=PACK),
+                in_=w2_raw[:].bitcast(U16).rearrange("p (m i) -> p m i", i=PACK),
+            )
+            wsc = keep.tile([P, KP], U8, name="wsc%d" % b, align_bytes=64)
+            nc.vector.tensor_copy(
+                out=wsc[:].rearrange("p (i m) -> p m i", i=PACK),
+                in_=ws_raw[:, b * KP:(b + 1) * KP].rearrange("p (m i) -> p m i", i=PACK),
+            )
+            return w2c, w3c, wsc
+
+        packed = {0: deal_packed(0, *w23_raw)}
+
+        w1_raw = load_weight(w1, 1, "stage_a")
+        w23_raw = load_packed(1)
+        ribbon_sb = keep.tile([P, NT, PICK], F32, name="ribbon_sb", tag="big")
+        nc.sync.dma_start(
+            ribbon_sb[:].rearrange("p (b i) m -> p b (i m)", i=PACK), ribbon.rearrange("(b p i) m -> p b (i m)", b=NB, i=PACK)
+        )
+
+        best = [keep.tile([P, S], F32, name="best%d" % t) for t in range(NT)]
+        picked = [keep.tile([P, PICK], F32, name="picked%d" % t) for t in range(NT)]
+        x_grouped = [keep.tile([P, PICK * PACK], BF16, name="x_grouped%d" % b, align_bytes=64) for b in range(NB)]
+        x_planes = keep.tile([P, PACK, PICK], BF16, name="x_planes")
+        xq = {}
+        w4q = {}
+
+        def first_stage(t):
+            b, i = divmod(t, PACK)
+            cols = slice(i * P, (i + 1) * P)
+            w1c, w1s = w1q[b]
+            w2c, w3c, wsc = packed[b]
+            held = []
+            for hf in range(S // BANK):
+                rhs = v_w[hf][:].bitcast(FP8X4)
+                rhs_scale = v_s[:, hf * BANK:(hf + 1) * BANK]
+                banks = [psum.tile([P, BANK], F32, name="bank", tag="bank") for n in range(3)]
+                nc.tensor.matmul_mx(out=banks[0][:], lhsT=w1c[:, cols].bitcast(FP8X4), lhsT_scale=w1s[:, cols],
+                                    rhs=rhs, rhs_scale=rhs_scale, start=True, stop=True)
+                nc.tensor.matmul_mx(out=banks[1][:], lhsT=w2c[:, 2 * i * P:2 * (i + 1) * P].bitcast(FP4X4), lhsT_scale=wsc[:, cols],
+                                    rhs=rhs, rhs_scale=rhs_scale, start=True, stop=True)
+                nc.tensor.matmul_mx(out=banks[2][:], lhsT=w3c[:, cols].bitcast(FP8X4), lhsT_scale=wsc[W3_ROW:P, cols],
+                                    rhs=rhs, rhs_scale=rhs_scale, start=True, stop=True)
+                one = ring.tile([P, BANK], F32, name="one", tag="one")
+                nc.scalar.copy(out=one[:], in_=banks[0][:])
+                two = ring.tile([P, BANK], F32, name="two", tag="two")
+                nc.vector.tensor_tensor(two[:], banks[1][:], one[:], ALU.max)
+                held.append((banks[2], two))
+            for hf in range(S // BANK):
+                nc.vector.tensor_tensor(best[t][:, hf * BANK:(hf + 1) * BANK], held[hf][0][:], held[hf][1][:], ALU.max)
+
+        def pick(t, c0=0, c1=PICK):
+            b, i = divmod(t, PACK)
+            nc.vector.tensor_copy(picked[t][:, c0:c1], best[t][:].indirect(p1[:, c0 // 16:c1 // 16]))
+            if b == 0:
+                dst = x_planes[:]
+            else:
+                dst = x_grouped[b][:].rearrange("p (m i) -> p i m", i=PACK)
+            nc.scalar.activation(out=dst[:, i, c0:c1], in_=picked[t][:, c0:c1], func=ACT.Copy, scale=gain_sb[:, t:t + 1])
+
+        def weave_planes():
+            dst = x_grouped[0][:].rearrange("p (c e i) -> p c i e", e=4, i=PACK)
+            src = x_planes[:].rearrange("p i (c e) -> p c i e", e=4)
+            step = PICK // 4 // 4
+            for s in range(4):
+                nc.scalar.copy(out=dst[:, s * step:(s + 1) * step], in_=src[:, s * step:(s + 1) * step])
+
+        def w4_part(a, b, stage):
+            raw = load_weight(w4[a * KP:(a + 1) * KP, :], b, stage)
+            return round_weight(raw, 4)
+
+        first_stage(0)
+        first_stage(1)
+        w1_grouped = round_weight(w1_raw, 4)
+        packed[1] = deal_packed(1, *w23_raw)
+        wgo_sb = keep.tile([P, PACK, PICK], F32, name="wgo_sb", tag="stage_d")
+        for q in range(4):
+            nc.sync.dma_start(wgo_sb[32 * q:32 * q + 32].rearrange("p i m -> p (i m)"), wgo.rearrange("(p i) m -> p (i m)", i=PACK))
+        pick(0)
+        first_stage(2)
+        pick(1)
+        w1q[1] = quantise(w1_grouped, "w1q1")
+        first_stage(3)
+        pick(2)
+        g40 = w4_part(0, 0, "stage_b")
+        first_stage(4)
+        pick(3)
+        weave_planes()
+        first_stage(5)
+        pick(4)
+        w4q[0, 0] = quantise(g40, "w4q00")
+        g41 = w4_part(1, 0, "stage_c")
+        first_stage(6)
+        pick(5)
+        xq[0] = quantise(x_grouped[0], "xq0")
+        first_stage(7)
+        pick(6)
+        w4q[1, 0] = quantise(g41, "w4q10")
+        xq[1] = mx_tiles("xq1")
+        halves = ((0, PICK // 2), (PICK // 2, PICK))
+        for c0, c1 in halves:
+            pick(7, c0, c1)
+        for c0, c1 in halves:
+            quantise_cols(xq[1], x_grouped[1], c0, c1)
+
+        out_rows = out.rearrange("(b p i) j -> b i p j", b=NB, i=PACK)
+        result, toned, summed = {}, {}, {}
+
+        def scale_all(t):
+            result[t] = ring.tile([P, S], F32, name="result", tag="result", bufs=4)
+            nc.scalar.activation(out=result[t][:], in_=best[t][:], func=ACT.Copy, scale=gs[:, t:t + 1])
+
+        def second_stage(t, c0=0, c1=PICK):
+            b, i = divmod(t, PACK)
+            cols = slice(i * P, (i + 1) * P)
+            bank = psum.tile([P, c1 - c0], F32, name="bank", tag="bank")
+            for a in range(NB):
+                wc, wsc = w4q[a, b]
+                xc, xs = xq[a]
+                nc.tensor.matmul_mx(out=bank[:], lhsT=wc[:, cols].bitcast(FP8X4), lhsT_scale=wsc[:, cols],
+                                    rhs=xc[:, c0:c1].bitcast(FP8X4), rhs_scale=xs[:, c0:c1], start=(a == 0), stop=(a == NB - 1))
+            th = ring.tile([P, c1 - c0], F32, name="th", tag="one")
+            nc.scalar.activation(out=th[:], in_=bank[:], func=ACT.Tanh)
+            toned[t, c0] = ring.tile([P, c1 - c0], F32, name="toned", tag="two")
+            nc.vector.tensor_tensor(toned[t, c0][:], th[:], ribbon_sb[:, t, c0:c1], ALU.mult)
+
+        def add_skip(t, c0=0, c1=PICK):
+            summed[t, c0] = ring.tile([P, c1 - c0], F32, name="summed", tag="summed")
+            nc.vector.scalar_tensor_tensor(summed[t, c0][:], picked[t][:, c0:c1], gs[:, t:t + 1], toned[t, c0][:], ALU.mult, ALU.add)
+
+        def put(t, c0=0, c1=PICK):
+            nc.vector.tensor_tensor(result[t][:].indirect(p1[:, c0 // 16:c1 // 16]), summed[t, c0][:], wgo_sb[:, t % PACK, c0:c1], ALU.mult)
+
+        def store(t):
+            b, i = divmod(t, PACK)
+            nc.sync.dma_start(out_rows[b, i], result[t][:])
+
+        late = {0: w4_part(0, 1, "stage_a")}
+        w4q[0, 1] = quantise(late[0], "w4q01")
+        scale_all(0)
+        for c0, c1 in halves:
+            second_stage(0, c0, c1)
+        for c0, c1 in halves:
+            add_skip(0, c0, c1)
+        put(0, *halves[0])
+        scale_all(1)
+        second_stage(1)
+        put(0, *halves[1])
+        store(0)
+        late[1] = w4_part(1, 1, "stage_b")
+        for t in range(1, NT):
+            add_skip(t)
+            if t == 1:
+                w4q[1, 1] = quantise(late[1], "w4q11")
+            if t + 1 < NT:
+                scale_all(t + 1)
+                second_stage(t + 1)
+            put(t)
+            store(t)

@@ -40,31 +40,39 @@ def tile_list_printhead_dot_features_kernel(
         p1 = lists.tile([P, PICK // 16], U16, name="p1")
         nc.sync.dma_start(p1[:], pos1)
 
-        def load_weight(src_rows, b, stage):
-            raw = keep.tile([P, PACK, KP], F32, name="raw", tag=stage)
+        def load_weight(src_rows, b, stage, align=None):
+            raw = keep.tile([P, PACK, KP], F32, name="raw", tag=stage, align_bytes=align)
             nc.sync.dma_start(raw[:], src_rows[:, b * KP:(b + 1) * KP].rearrange("(p j) c -> p j c", j=PACK))
             return raw
 
-        def round_weight(raw, pieces):
-            grouped = ring.tile([P, PACK * KP], BF16, name="grouped", tag="grouped", bufs=3, align_bytes=64)
-            dst = grouped[:].rearrange("p (t m j) -> p m t j", t=PACK, j=PACK)
+        def round_into(grouped, a, raw, pair, on_gpsimd=False):
+            dst = grouped[:, a * 2 * KP:(a + 1) * 2 * KP].rearrange("p (t m j) -> p m t j", t=2, j=PACK)
             src = raw[:].rearrange("p j (m t) -> p m t j", t=PACK)
-            step = P // pieces
-            for s in range(pieces):
-                nc.scalar.copy(out=dst[:, s * step:(s + 1) * step], in_=src[:, s * step:(s + 1) * step])
+            src = src[:, :, 2 * pair:2 * pair + 2, :]
+            if on_gpsimd:
+                for m0 in range(0, P, P // 2):
+                    nc.gpsimd.tensor_scalar(dst[:, m0:m0 + P // 2], src[:, m0:m0 + P // 2], 1.0, 0.0, ALU.mult, ALU.add)
+            else:
+                nc.scalar.copy(out=dst, in_=src)
+
+        def round_pair(raws, pair, tag):
+            grouped = keep.tile([P, len(raws) * 2 * KP], BF16, name="grouped", tag=tag, align_bytes=64)
+            for a, raw in enumerate(raws):
+                round_into(grouped, a, raw, pair)
             return grouped
 
-        def mx_tiles(name):
-            codes = keep.tile([P, KP], U32, name=name + "_codes", align_bytes=64)
-            scales = keep.tile([P, KP], U8, name=name + "_scales", align_bytes=64)
+        def mx_tiles(name, width, tag=None):
+            codes = keep.tile([P, width], U32, name=name + "_codes", tag=tag or name + "_codes", align_bytes=64)
+            scales = keep.tile([P, width], U8, name=name + "_scales", align_bytes=64)
             return codes, scales
 
         def quantise_cols(tiles, grouped, c0, c1):
-            nc.vector.quantize_mx(out=tiles[0][:, c0:c1].bitcast(FP8X4), scales=tiles[1][:, c0:c1], in_=grouped[:, PACK * c0:PACK * c1])
+            nc.vector.quantize_mx(out=tiles[0][:, c0:c1].bitcast(FP8X4), scales=tiles[1][:, c0:c1], in_=grouped[:])
 
-        def quantise(grouped, name):
-            tiles = mx_tiles(name)
-            quantise_cols(tiles, grouped, 0, KP)
+        def quantise(grouped, name, tag=None):
+            width = grouped.shape[1] // PACK
+            tiles = mx_tiles(name, width, tag)
+            quantise_cols(tiles, grouped, 0, width)
             return tiles
 
         gain_sb = keep.tile([P, NT], F32, name="gain_sb")
@@ -91,7 +99,7 @@ def tile_list_printhead_dot_features_kernel(
         nc.vector.memset(tab_s[:].bitcast(I32), 0)
         for q in range(4):
             nc.scalar.dma_start(tab_s[32 * q:32 * q + 4, :].bitcast(I32), tab_scales[0, 4 * q:4 * q + 4, :].bitcast(I32))
-        ws_raw = keep.tile([P, H], U8, name="ws_raw")
+        ws_raw = keep.tile([P, H], U8, name="ws_raw", tag="ws_raw")
         nc.gpsimd.memset(ws_raw[:].bitcast(I32), 0)
         for q in range(4):
             r0 = 32 * q + W3_ROW
@@ -100,10 +108,10 @@ def tile_list_printhead_dot_features_kernel(
             queue = nc.gpsimd if q == 0 else nc.sync
             queue.dma_start(ws_raw[32 * q:32 * q + 4, :].bitcast(I32), w2_scales[0, 4 * q:4 * q + 4, :].bitcast(I32))
 
-        w1_grouped = round_weight(w1_raw, 1)
+        w1_grouped = [round_pair([w1_raw], u, "w1_grouped%d" % u) for u in range(2)]
         v_s = keep.tile([P, S], U8, name="v_s", align_bytes=64)
         nc.vector.tensor_copy(v_s[:], tab_s[:].indirect(idx[:]))
-        w1q = {0: quantise(w1_grouped, "w1q0")}
+        w1q = {u: quantise(w1_grouped[u], "w1q%d" % u) for u in range(2)}
         v_w = []
         for hf in range(S // BANK):
             vw = keep.tile([P, BANK], U32, name="v_w%d" % hf, align_bytes=64)
@@ -130,120 +138,162 @@ def tile_list_printhead_dot_features_kernel(
 
         w1_raw = load_weight(w1, 1, "stage_a")
         w23_raw = load_packed(1)
-        ribbon_sb = keep.tile([P, NT, PICK], F32, name="ribbon_sb", tag="big")
-        nc.sync.dma_start(
-            ribbon_sb[:].rearrange("p (b i) m -> p b (i m)", i=PACK), ribbon.rearrange("(b p i) m -> p b (i m)", b=NB, i=PACK)
-        )
+        w4_raw = {(0, 0): load_weight(w4[0:KP, :], 0, "stage_b"), (1, 0): load_weight(w4[KP:2 * KP, :], 0, "big")}
 
-        best = [keep.tile([P, S], F32, name="best%d" % t) for t in range(NT)]
+        best = [keep.tile([P, S], F32, name="best%d" % t, tag="best%d" % t, align_bytes=64) for t in range(NT)]
         picked = [keep.tile([P, PICK], F32, name="picked%d" % t) for t in range(NT)]
-        x_grouped = [keep.tile([P, PICK * PACK], BF16, name="x_grouped%d" % b, align_bytes=64) for b in range(NB)]
-        x_planes = keep.tile([P, PACK, PICK], BF16, name="x_planes")
+        halves = ((0, PICK // 2), (PICK // 2, PICK))
+        x_first = keep.tile([P, PICK * PACK], BF16, name="x_first", align_bytes=64)
+        x_last = {c0: keep.tile([P, (c1 - c0) * PACK], BF16, name="x_last%d" % c0, tag="x_last%d" % c0, align_bytes=64) for c0, c1 in halves}
+        x_planes = [keep.tile([P, PACK, PICK], BF16, name="x_planes%d" % b, tag="x_planes%d" % b, align_bytes=64) for b in range(NB)]
         xq = {}
         w4q = {}
 
+        ones = {}
+
+        def product(bank, lhsT, lhsT_scale, hf):
+            nc.tensor.matmul_mx(out=bank[:], lhsT=lhsT, lhsT_scale=lhsT_scale, rhs=v_w[hf][:].bitcast(FP8X4),
+                                rhs_scale=v_s[:, hf * BANK:(hf + 1) * BANK], start=True, stop=True)
+
+        def lead(t):
+            w1c, w1s = w1q[t // 2]
+            cols = slice((t % 2) * P, (t % 2 + 1) * P)
+            for hf in range(S // BANK):
+                bank = psum.tile([P, BANK], F32, name="lead_bank", tag="lead_bank", bufs=2)
+                product(bank, w1c[:, cols].bitcast(FP8X4), w1s[:, cols], hf)
+                ones[t, hf] = ring.tile([P, BANK], F32, name="one", tag="one", bufs=5)
+                nc.scalar.copy(out=ones[t, hf][:], in_=bank[:])
+
         def first_stage(t):
+            if t + 1 < NT:
+                lead(t + 1)
             b, i = divmod(t, PACK)
             cols = slice(i * P, (i + 1) * P)
-            w1c, w1s = w1q[b]
             w2c, w3c, wsc = packed[b]
             held = []
             for hf in range(S // BANK):
-                rhs = v_w[hf][:].bitcast(FP8X4)
-                rhs_scale = v_s[:, hf * BANK:(hf + 1) * BANK]
-                banks = [psum.tile([P, BANK], F32, name="bank", tag="bank") for n in range(3)]
-                nc.tensor.matmul_mx(out=banks[0][:], lhsT=w1c[:, cols].bitcast(FP8X4), lhsT_scale=w1s[:, cols],
-                                    rhs=rhs, rhs_scale=rhs_scale, start=True, stop=True)
-                nc.tensor.matmul_mx(out=banks[1][:], lhsT=w2c[:, 2 * i * P:2 * (i + 1) * P].bitcast(FP4X4), lhsT_scale=wsc[:, cols],
-                                    rhs=rhs, rhs_scale=rhs_scale, start=True, stop=True)
-                nc.tensor.matmul_mx(out=banks[2][:], lhsT=w3c[:, cols].bitcast(FP8X4), lhsT_scale=wsc[W3_ROW:P, cols],
-                                    rhs=rhs, rhs_scale=rhs_scale, start=True, stop=True)
-                one = ring.tile([P, BANK], F32, name="one", tag="one")
-                nc.scalar.copy(out=one[:], in_=banks[0][:])
+                banks = [psum.tile([P, BANK], F32, name="bank", tag="bank", bufs=6) for n in range(2)]
+                product(banks[0], w2c[:, 2 * i * P:2 * (i + 1) * P].bitcast(FP4X4), wsc[:, cols], hf)
+                product(banks[1], w3c[:, cols].bitcast(FP8X4), wsc[W3_ROW:P, cols], hf)
                 two = ring.tile([P, BANK], F32, name="two", tag="two")
-                nc.vector.tensor_tensor(two[:], banks[1][:], one[:], ALU.max)
-                held.append((banks[2], two))
+                nc.vector.tensor_tensor(two[:], banks[0][:], ones[t, hf][:], ALU.max)
+                held.append((banks[1], two))
             for hf in range(S // BANK):
                 nc.vector.tensor_tensor(best[t][:, hf * BANK:(hf + 1) * BANK], held[hf][0][:], held[hf][1][:], ALU.max)
 
         def pick(t, c0=0, c1=PICK):
             b, i = divmod(t, PACK)
             nc.vector.tensor_copy(picked[t][:, c0:c1], best[t][:].indirect(p1[:, c0 // 16:c1 // 16]))
-            if b == 0:
-                dst = x_planes[:]
+            if t < NT - 1:
+                dst = x_planes[b][:, i, c0:c1]
             else:
-                dst = x_grouped[b][:].rearrange("p (m i) -> p i m", i=PACK)
-            nc.scalar.activation(out=dst[:, i, c0:c1], in_=picked[t][:, c0:c1], func=ACT.Copy, scale=gain_sb[:, t:t + 1])
+                dst = x_last[c0][:].rearrange("p (m i) -> p i m", i=PACK)[:, i, :]
+            nc.scalar.activation(out=dst, in_=picked[t][:, c0:c1], func=ACT.Copy, scale=gain_sb[:, t:t + 1])
 
-        def weave_planes():
-            dst = x_grouped[0][:].rearrange("p (c e i) -> p c i e", e=4, i=PACK)
-            src = x_planes[:].rearrange("p i (c e) -> p c i e", e=4)
-            step = PICK // 4 // 4
-            for s in range(4):
-                nc.scalar.copy(out=dst[:, s * step:(s + 1) * step], in_=src[:, s * step:(s + 1) * step])
-
-        def w4_part(a, b, stage):
-            raw = load_weight(w4[a * KP:(a + 1) * KP, :], b, stage)
-            return round_weight(raw, 4)
-
-        first_stage(0)
-        first_stage(1)
-        w1_grouped = round_weight(w1_raw, 4)
-        packed[1] = deal_packed(1, *w23_raw)
-        wgo_sb = keep.tile([P, PACK, PICK], F32, name="wgo_sb", tag="stage_d")
-        for q in range(4):
-            nc.sync.dma_start(wgo_sb[32 * q:32 * q + 32].rearrange("p i m -> p (i m)"), wgo.rearrange("(p i) m -> p (i m)", i=PACK))
-        pick(0)
-        first_stage(2)
-        pick(1)
-        w1q[1] = quantise(w1_grouped, "w1q1")
-        first_stage(3)
-        pick(2)
-        g40 = w4_part(0, 0, "stage_b")
-        first_stage(4)
-        pick(3)
-        weave_planes()
-        first_stage(5)
-        pick(4)
-        w4q[0, 0] = quantise(g40, "w4q00")
-        g41 = w4_part(1, 0, "stage_c")
-        first_stage(6)
-        pick(5)
-        xq[0] = quantise(x_grouped[0], "xq0")
-        first_stage(7)
-        pick(6)
-        w4q[1, 0] = quantise(g41, "w4q10")
-        xq[1] = mx_tiles("xq1")
-        halves = ((0, PICK // 2), (PICK // 2, PICK))
-        for c0, c1 in halves:
-            pick(7, c0, c1)
-        for c0, c1 in halves:
-            quantise_cols(xq[1], x_grouped[1], c0, c1)
+        def weave(dst, b, planes, c0, c1):
+            src = x_planes[b][:, 0:planes, c0:c1].rearrange("p i (c e) -> p c i e", e=4)
+            nc.scalar.copy(out=dst.rearrange("p (c e i) -> p c i e", e=4, i=PACK)[:, :, 0:planes, :], in_=src)
 
         out_rows = out.rearrange("(b p i) j -> b i p j", b=NB, i=PACK)
         result, toned, summed = {}, {}, {}
+        result_tags = ["result", "hold2", "hold3"] + ["best%d" % (t - 2) for t in range(3, NT)]
 
         def scale_all(t):
-            result[t] = ring.tile([P, S], F32, name="result", tag="result", bufs=4)
-            nc.scalar.activation(out=result[t][:], in_=best[t][:], func=ACT.Copy, scale=gs[:, t:t + 1])
+            result[t] = keep.tile([P, S], F32, name="result", tag=result_tags[t], align_bytes=64)
+            if t == 0:
+                nc.gpsimd.tensor_scalar(result[t][:], best[t][:], gs[:, t:t + 1], 0.0, ALU.mult, ALU.add)
+            else:
+                nc.scalar.activation(out=result[t][:], in_=best[t][:], func=ACT.Copy, scale=gs[:, t:t + 1])
+
+        lead(0)
+        first_stage(0)
+        packed[1] = deal_packed(1, *w23_raw)
+        ribbon_rows = ribbon.rearrange("(b p i) m -> b p (i m)", b=NB, i=PACK)
+        ribbon_sb = []
+        for b, stage in enumerate(("stage_c", "ws_raw")):
+            part = keep.tile([P, PACK, PICK], F32, name="ribbon_sb", tag=stage)
+            nc.sync.dma_start(part[:].rearrange("p i m -> p (i m)"), ribbon_rows[b])
+            ribbon_sb.append(part)
+        wgo_sb = keep.tile([P, PACK, PICK], F32, name="wgo_sb", tag="stage_d")
+        for q in range(4):
+            nc.sync.dma_start(wgo_sb[32 * q:32 * q + 32].rearrange("p i m -> p (i m)"), wgo.rearrange("(p i) m -> p (i m)", i=PACK))
+        w1_grouped = {2: round_pair([w1_raw], 0, "w1_grouped0")}
+        first_stage(1)
+        pick(0)
+        scale_all(0)
+        w1_grouped[3] = round_pair([w1_raw], 1, "w1_grouped1")
+        w4_raw[0, 1] = load_weight(w4[0:KP, :], 1, "stage_a")
+        w4_grouped = [keep.tile([P, 4 * KP], BF16, name="w4_grouped%d" % u, align_bytes=64) for u in range(4)]
+        round_into(w4_grouped[0], 0, w4_raw[0, 0], 0)
+        w1q[2] = quantise(w1_grouped[2], "w1q2")
+        first_stage(2)
+        pick(1)
+        w1q[3] = quantise(w1_grouped[3], "w1q3")
+        w4_raw[1, 1] = load_weight(w4[KP:2 * KP, :], 1, "w1_grouped1", 64)
+        round_into(w4_grouped[0], 1, w4_raw[1, 0], 0)
+        for u in (1, 0):
+            for a in range(NB):
+                round_into(w4_grouped[2 + u], a, w4_raw[a, 1], u, True)
+        first_stage(3)
+        pick(2)
+        round_into(w4_grouped[1], 0, w4_raw[0, 0], 1)
+        first_stage(4)
+        pick(3)
+        round_into(w4_grouped[1], 1, w4_raw[1, 0], 1)
+        for c0 in range(0, PICK // 2, P):
+            weave(x_first[:, PACK * c0:PACK * (c0 + P)], 0, PACK, c0, c0 + P)
+        first_stage(5)
+        pick(4)
+        for c0 in range(PICK // 2, PICK, P):
+            weave(x_first[:, PACK * c0:PACK * (c0 + P)], 0, PACK, c0, c0 + P)
+        first_stage(6)
+        pick(5)
+        xq[0] = quantise(x_first, "xq0")
+        w4q[3] = quantise(w4_grouped[3], "w4q3")
+        pick(6)
+        first_stage(7)
+        for c0, c1 in halves:
+            weave(x_last[c0][:], 1, PACK - 1, c0, c1)
+        xq[1] = mx_tiles("xq1", PICK)
+        for c0, c1 in halves:
+            pick(7, c0, c1)
+        w4q[0] = quantise(w4_grouped[0], "w4q0", "x_planes1")
+        for c0, c1 in halves:
+            quantise_cols(xq[1], x_last[c0], c0, c1)
+        w4q[1] = quantise(w4_grouped[1], "w4q1", "x_last0")
+        w4q[2] = quantise(w4_grouped[2], "w4q2", "x_last256")
 
         def second_stage(t, c0=0, c1=PICK):
-            b, i = divmod(t, PACK)
-            cols = slice(i * P, (i + 1) * P)
-            bank = psum.tile([P, c1 - c0], F32, name="bank", tag="bank")
+            bank = psum.tile([P, c1 - c0], F32, name="bank", tag="bank", bufs=6)
+            wc, wsc = w4q[t // 2]
             for a in range(NB):
-                wc, wsc = w4q[a, b]
+                cols = slice((2 * a + t % 2) * P, (2 * a + t % 2 + 1) * P)
                 xc, xs = xq[a]
                 nc.tensor.matmul_mx(out=bank[:], lhsT=wc[:, cols].bitcast(FP8X4), lhsT_scale=wsc[:, cols],
                                     rhs=xc[:, c0:c1].bitcast(FP8X4), rhs_scale=xs[:, c0:c1], start=(a == 0), stop=(a == NB - 1))
-            th = ring.tile([P, c1 - c0], F32, name="th", tag="one")
+            if t == 0:
+                th = keep.tile([P, c1 - c0], F32, name="th", tag="hold%d" % (c0 > 0), align_bytes=64)
+            else:
+                th = ring.tile([P, c1 - c0], F32, name="th", tag="one", bufs=5)
             nc.scalar.activation(out=th[:], in_=bank[:], func=ACT.Tanh)
-            toned[t, c0] = ring.tile([P, c1 - c0], F32, name="toned", tag="two")
-            nc.vector.tensor_tensor(toned[t, c0][:], th[:], ribbon_sb[:, t, c0:c1], ALU.mult)
+            curved[t, c0] = th
+
+        def tone(t, c0=0, c1=PICK):
+            th = curved[t, c0]
+            engine = nc.vector
+            if t == 0:
+                toned[t, c0] = keep.tile([P, c1 - c0], F32, name="toned", tag="hold%d" % (2 + (c0 > 0)), align_bytes=64)
+            else:
+                toned[t, c0] = ring.tile([P, c1 - c0], F32, name="toned", tag="two")
+            engine.tensor_tensor(toned[t, c0][:], th[:], ribbon_sb[t // PACK][:, t % PACK, c0:c1], ALU.mult)
 
         def add_skip(t, c0=0, c1=PICK):
-            summed[t, c0] = ring.tile([P, c1 - c0], F32, name="summed", tag="summed")
+            hold = 4 + (c0 > 0) if t == 0 else (0, 1, 4)[(t - 1) % 3]
+            summed[t, c0] = keep.tile([P, c1 - c0], F32, name="summed", tag="hold%d" % hold, align_bytes=64)
             nc.vector.scalar_tensor_tensor(summed[t, c0][:], picked[t][:, c0:c1], gs[:, t:t + 1], toned[t, c0][:], ALU.mult, ALU.add)
+
+        def weigh(t, c0=0, c1=PICK):
+            return
 
         def put(t, c0=0, c1=PICK):
             nc.vector.tensor_tensor(result[t][:].indirect(p1[:, c0 // 16:c1 // 16]), summed[t, c0][:], wgo_sb[:, t % PACK, c0:c1], ALU.mult)
@@ -252,25 +302,23 @@ def tile_list_printhead_dot_features_kernel(
             b, i = divmod(t, PACK)
             nc.sync.dma_start(out_rows[b, i], result[t][:])
 
-        late = {0: w4_part(0, 1, "stage_a")}
-        w4q[0, 1] = quantise(late[0], "w4q01")
-        scale_all(0)
+        weighed, curved = {}, {}
         for c0, c1 in halves:
             second_stage(0, c0, c1)
-        for c0, c1 in halves:
-            add_skip(0, c0, c1)
-        put(0, *halves[0])
-        scale_all(1)
         second_stage(1)
-        put(0, *halves[1])
+        second_stage(2)
+        for step in (tone, add_skip, weigh, put):
+            for c0, c1 in halves:
+                step(0, c0, c1)
         store(0)
-        late[1] = w4_part(1, 1, "stage_b")
+        tone(1)
         for t in range(1, NT):
             add_skip(t)
-            if t == 1:
-                w4q[1, 1] = quantise(late[1], "w4q11")
+            if t + 2 < NT:
+                second_stage(t + 2)
             if t + 1 < NT:
-                scale_all(t + 1)
-                second_stage(t + 1)
+                tone(t + 1)
+            weigh(t)
+            scale_all(t)
             put(t)
             store(t)

@@ -45,15 +45,11 @@ def tile_list_printhead_dot_features_kernel(
             nc.sync.dma_start(raw[:], src_rows[:, b * KP:(b + 1) * KP].rearrange("(p j) c -> p j c", j=PACK))
             return raw
 
-        def round_into(grouped, a, raw, pair, on_gpsimd=False):
+        def round_into(grouped, a, raw, pair):
             dst = grouped[:, a * 2 * KP:(a + 1) * 2 * KP].rearrange("p (t m j) -> p m t j", t=2, j=PACK)
             src = raw[:].rearrange("p j (m t) -> p m t j", t=PACK)
             src = src[:, :, 2 * pair:2 * pair + 2, :]
-            if on_gpsimd:
-                for m0 in range(0, P, P // 2):
-                    nc.gpsimd.tensor_scalar(dst[:, m0:m0 + P // 2], src[:, m0:m0 + P // 2], 1.0, 0.0, ALU.mult, ALU.add)
-            else:
-                nc.scalar.copy(out=dst, in_=src)
+            nc.scalar.copy(out=dst, in_=src)
 
         def round_pair(raws, pair, tag):
             grouped = keep.tile([P, len(raws) * 2 * KP], BF16, name="grouped", tag=tag, align_bytes=64)
@@ -143,7 +139,7 @@ def tile_list_printhead_dot_features_kernel(
         best = [keep.tile([P, S], F32, name="best%d" % t, tag="best%d" % t, align_bytes=64) for t in range(NT)]
         picked = [keep.tile([P, PICK], F32, name="picked%d" % t) for t in range(NT)]
         halves = ((0, PICK // 2), (PICK // 2, PICK))
-        x_first = keep.tile([P, PICK * PACK], BF16, name="x_first", align_bytes=64)
+        x_first = keep.tile([P, PICK * PACK], BF16, name="x_first", tag="x_first", align_bytes=64)
         x_last = {c0: keep.tile([P, (c1 - c0) * PACK], BF16, name="x_last%d" % c0, tag="x_last%d" % c0, align_bytes=64) for c0, c1 in halves}
         x_planes = [keep.tile([P, PACK, PICK], BF16, name="x_planes%d" % b, tag="x_planes%d" % b, align_bytes=64) for b in range(NB)]
         xq = {}
@@ -161,12 +157,10 @@ def tile_list_printhead_dot_features_kernel(
             for hf in range(S // BANK):
                 bank = psum.tile([P, BANK], F32, name="lead_bank", tag="lead_bank", bufs=2)
                 product(bank, w1c[:, cols].bitcast(FP8X4), w1s[:, cols], hf)
-                ones[t, hf] = ring.tile([P, BANK], F32, name="one", tag="one", bufs=5)
+                ones[t, hf] = ring.tile([P, BANK], F32, name="one", tag="one", bufs=8)
                 nc.scalar.copy(out=ones[t, hf][:], in_=bank[:])
 
         def first_stage(t):
-            if t + 1 < NT:
-                lead(t + 1)
             b, i = divmod(t, PACK)
             cols = slice(i * P, (i + 1) * P)
             w2c, w3c, wsc = packed[b]
@@ -176,14 +170,16 @@ def tile_list_printhead_dot_features_kernel(
                 product(banks[0], w2c[:, 2 * i * P:2 * (i + 1) * P].bitcast(FP4X4), wsc[:, cols], hf)
                 product(banks[1], w3c[:, cols].bitcast(FP8X4), wsc[W3_ROW:P, cols], hf)
                 two = ring.tile([P, BANK], F32, name="two", tag="two")
-                nc.vector.tensor_tensor(two[:], banks[0][:], ones[t, hf][:], ALU.max)
+                nc.vector.tensor_tensor(two[:], ones[t, hf][:], banks[0][:], ALU.max)
                 held.append((banks[1], two))
             for hf in range(S // BANK):
-                nc.vector.tensor_tensor(best[t][:, hf * BANK:(hf + 1) * BANK], held[hf][0][:], held[hf][1][:], ALU.max)
+                nc.vector.tensor_tensor(best[t][:, hf * BANK:(hf + 1) * BANK], held[hf][1][:], held[hf][0][:], ALU.max)
 
         def pick(t, c0=0, c1=PICK):
-            b, i = divmod(t, PACK)
             nc.vector.tensor_copy(picked[t][:, c0:c1], best[t][:].indirect(p1[:, c0 // 16:c1 // 16]))
+
+        def round_picked(t, c0=0, c1=PICK):
+            b, i = divmod(t, PACK)
             if t < NT - 1:
                 dst = x_planes[b][:, i, c0:c1]
             else:
@@ -196,74 +192,60 @@ def tile_list_printhead_dot_features_kernel(
 
         out_rows = out.rearrange("(b p i) j -> b i p j", b=NB, i=PACK)
         result, toned, summed = {}, {}, {}
-        result_tags = ["result", "hold2", "hold3"] + ["best%d" % (t - 2) for t in range(3, NT)]
+        result_tags = ["x_last256", "hold2", "hold3"] + ["best%d" % (t - 2) for t in range(3, NT)]
 
         def scale_all(t):
             result[t] = keep.tile([P, S], F32, name="result", tag=result_tags[t], align_bytes=64)
-            if t == 0:
-                nc.gpsimd.tensor_scalar(result[t][:], best[t][:], gs[:, t:t + 1], 0.0, ALU.mult, ALU.add)
-            else:
-                nc.scalar.activation(out=result[t][:], in_=best[t][:], func=ACT.Copy, scale=gs[:, t:t + 1])
+            nc.scalar.activation(out=result[t][:], in_=best[t][:], func=ACT.Copy, scale=gs[:, t:t + 1])
 
-        lead(0)
-        first_stage(0)
+        for t in range(PACK):
+            lead(t)
         packed[1] = deal_packed(1, *w23_raw)
+        for u in range(2):
+            w1q[2 + u] = quantise(round_pair([w1_raw], u, "w1_grouped%d" % u), "w1q%d" % (2 + u))
         ribbon_rows = ribbon.rearrange("(b p i) m -> b p (i m)", b=NB, i=PACK)
         ribbon_sb = []
         for b, stage in enumerate(("stage_c", "ws_raw")):
-            part = keep.tile([P, PACK, PICK], F32, name="ribbon_sb", tag=stage)
-            nc.sync.dma_start(part[:].rearrange("p i m -> p (i m)"), ribbon_rows[b])
+            part = keep.tile([P, PACK * PICK], F32, name="ribbon_sb", tag=stage)
+            nc.sync.dma_start(part[:], ribbon_rows[b])
             ribbon_sb.append(part)
         wgo_sb = keep.tile([P, PACK, PICK], F32, name="wgo_sb", tag="stage_d")
         for q in range(4):
             nc.sync.dma_start(wgo_sb[32 * q:32 * q + 32].rearrange("p i m -> p (i m)"), wgo.rearrange("(p i) m -> p (i m)", i=PACK))
-        w1_grouped = {2: round_pair([w1_raw], 0, "w1_grouped0")}
-        first_stage(1)
-        pick(0)
-        scale_all(0)
-        w1_grouped[3] = round_pair([w1_raw], 1, "w1_grouped1")
         w4_raw[0, 1] = load_weight(w4[0:KP, :], 1, "stage_a")
-        w4_grouped = [keep.tile([P, 4 * KP], BF16, name="w4_grouped%d" % u, align_bytes=64) for u in range(4)]
-        round_into(w4_grouped[0], 0, w4_raw[0, 0], 0)
-        w1q[2] = quantise(w1_grouped[2], "w1q2")
-        first_stage(2)
-        pick(1)
-        w1q[3] = quantise(w1_grouped[3], "w1q3")
         w4_raw[1, 1] = load_weight(w4[KP:2 * KP, :], 1, "w1_grouped1", 64)
-        round_into(w4_grouped[0], 1, w4_raw[1, 0], 0)
-        for u in (1, 0):
+        w4_grouped = [keep.tile([P, 4 * KP], BF16, name="w4_grouped%d" % u, tag="w4_grouped%d" % u, align_bytes=64) for u in range(2)]
+        for t in range(NT):
+            first_stage(t)
+            if t < PACK:
+                lead(t + PACK)
+            if 0 < t < NT - 1:
+                pick(t - 1)
+            if t == NT - 2:
+                pick(t)
+        for u in range(2):
             for a in range(NB):
-                round_into(w4_grouped[2 + u], a, w4_raw[a, 1], u, True)
-        first_stage(3)
-        pick(2)
-        round_into(w4_grouped[1], 0, w4_raw[0, 0], 1)
-        first_stage(4)
-        pick(3)
-        round_into(w4_grouped[1], 1, w4_raw[1, 0], 1)
-        for c0 in range(0, PICK // 2, P):
+                round_into(w4_grouped[u], a, w4_raw[a, 0], u)
+        for t in range(PACK):
+            round_picked(t)
+        for c0 in range(0, PICK, P):
             weave(x_first[:, PACK * c0:PACK * (c0 + P)], 0, PACK, c0, c0 + P)
-        first_stage(5)
-        pick(4)
-        for c0 in range(PICK // 2, PICK, P):
-            weave(x_first[:, PACK * c0:PACK * (c0 + P)], 0, PACK, c0, c0 + P)
-        first_stage(6)
-        pick(5)
         xq[0] = quantise(x_first, "xq0")
-        w4q[3] = quantise(w4_grouped[3], "w4q3")
-        pick(6)
-        first_stage(7)
+        for t in range(PACK, NT - 1):
+            round_picked(t)
         for c0, c1 in halves:
             weave(x_last[c0][:], 1, PACK - 1, c0, c1)
         xq[1] = mx_tiles("xq1", PICK)
         for c0, c1 in halves:
-            pick(7, c0, c1)
+            pick(NT - 1, c0, c1)
+            round_picked(NT - 1, c0, c1)
         w4q[0] = quantise(w4_grouped[0], "w4q0", "x_planes1")
         for c0, c1 in halves:
             quantise_cols(xq[1], x_last[c0], c0, c1)
         w4q[1] = quantise(w4_grouped[1], "w4q1", "x_last0")
-        w4q[2] = quantise(w4_grouped[2], "w4q2", "x_last256")
+        scale_all(0)
 
-        def second_stage(t, c0=0, c1=PICK):
+        def second_stage(th, t, c0=0, c1=PICK):
             bank = psum.tile([P, c1 - c0], F32, name="bank", tag="bank", bufs=6)
             wc, wsc = w4q[t // 2]
             for a in range(NB):
@@ -271,29 +253,17 @@ def tile_list_printhead_dot_features_kernel(
                 xc, xs = xq[a]
                 nc.tensor.matmul_mx(out=bank[:], lhsT=wc[:, cols].bitcast(FP8X4), lhsT_scale=wsc[:, cols],
                                     rhs=xc[:, c0:c1].bitcast(FP8X4), rhs_scale=xs[:, c0:c1], start=(a == 0), stop=(a == NB - 1))
-            if t == 0:
-                th = keep.tile([P, c1 - c0], F32, name="th", tag="hold%d" % (c0 > 0), align_bytes=64)
-            else:
-                th = ring.tile([P, c1 - c0], F32, name="th", tag="one", bufs=5)
-            nc.scalar.activation(out=th[:], in_=bank[:], func=ACT.Tanh)
-            curved[t, c0] = th
+            nc.scalar.activation(out=th, in_=bank[:], func=ACT.Tanh)
 
-        def tone(t, c0=0, c1=PICK):
-            th = curved[t, c0]
-            engine = nc.vector
-            if t == 0:
-                toned[t, c0] = keep.tile([P, c1 - c0], F32, name="toned", tag="hold%d" % (2 + (c0 > 0)), align_bytes=64)
-            else:
-                toned[t, c0] = ring.tile([P, c1 - c0], F32, name="toned", tag="two")
-            engine.tensor_tensor(toned[t, c0][:], th[:], ribbon_sb[t // PACK][:, t % PACK, c0:c1], ALU.mult)
+        def tone(th, t, c0, width, tag):
+            tile = keep.tile([P, width], F32, name="toned", tag=tag, align_bytes=64)
+            first = (t % PACK) * PICK + c0
+            nc.vector.tensor_tensor(tile[:], th, ribbon_sb[t // PACK][:, first:first + width], ALU.mult)
+            return tile
 
-        def add_skip(t, c0=0, c1=PICK):
-            hold = 4 + (c0 > 0) if t == 0 else (0, 1, 4)[(t - 1) % 3]
-            summed[t, c0] = keep.tile([P, c1 - c0], F32, name="summed", tag="hold%d" % hold, align_bytes=64)
-            nc.vector.scalar_tensor_tensor(summed[t, c0][:], picked[t][:, c0:c1], gs[:, t:t + 1], toned[t, c0][:], ALU.mult, ALU.add)
-
-        def weigh(t, c0=0, c1=PICK):
-            return
+        def add_skip(toned_part, t, c0, c1, tag):
+            summed[t, c0] = keep.tile([P, c1 - c0], F32, name="summed", tag=tag, align_bytes=64)
+            nc.vector.scalar_tensor_tensor(summed[t, c0][:], picked[t][:, c0:c1], gs[:, t:t + 1], toned_part, ALU.mult, ALU.add)
 
         def put(t, c0=0, c1=PICK):
             nc.vector.tensor_tensor(result[t][:].indirect(p1[:, c0 // 16:c1 // 16]), summed[t, c0][:], wgo_sb[:, t % PACK, c0:c1], ALU.mult)
@@ -302,23 +272,48 @@ def tile_list_printhead_dot_features_kernel(
             b, i = divmod(t, PACK)
             nc.sync.dma_start(out_rows[b, i], result[t][:])
 
-        weighed, curved = {}, {}
-        for c0, c1 in halves:
-            second_stage(0, c0, c1)
-        second_stage(1)
-        second_stage(2)
-        for step in (tone, add_skip, weigh, put):
-            for c0, c1 in halves:
-                step(0, c0, c1)
+        def curve_pair(u):
+            th = keep.tile([P, 2 * PICK], F32, name="th_pair", tag="w4_grouped%d" % ((u - 1) % 2), align_bytes=64)
+            for e in range(2):
+                second_stage(th[:, e * PICK:(e + 1) * PICK], 2 * u + e)
+            return th
+
+        half_th, half_toned = [], []
+        for n, (c0, c1) in enumerate(halves):
+            th = keep.tile([P, c1 - c0], F32, name="th", tag="hold%d" % n, align_bytes=64)
+            second_stage(th[:], 0, c0, c1)
+            half_th.append(th)
+        th1 = ring.tile([P, PICK], F32, name="th1", tag="two")
+        second_stage(th1[:], 1)
+        for n, (c0, c1) in enumerate(halves):
+            half_toned.append(tone(half_th[n][:], 0, c0, c1 - c0, "hold%d" % (2 + n)))
+        for n, (c0, c1) in enumerate(halves):
+            add_skip(half_toned[n][:], 0, c0, c1, "hold%d" % (4 + n))
+        put(0, *halves[0])
+        toned1 = tone(th1[:], 1, 0, PICK, "toned1")
+        put(0, *halves[1])
         store(0)
-        tone(1)
-        for t in range(1, NT):
-            add_skip(t)
-            if t + 2 < NT:
-                second_stage(t + 2)
-            if t + 1 < NT:
-                tone(t + 1)
-            weigh(t)
-            scale_all(t)
-            put(t)
-            store(t)
+        add_skip(toned1[:], 1, 0, PICK, "summed1")
+        th = curve_pair(1)
+        scale_all(1)
+        late = {u: round_pair([w4_raw[0, 1], w4_raw[1, 1]], u - 2, "hold%d" % (u + 2)) for u in (2,)}
+        toned_pair = tone(th[:], 2, 0, 2 * PICK, "x_first")
+        put(1)
+        store(1)
+        for u in range(1, NT // 2):
+            if u + 1 < NT // 2:
+                w4q[u + 1] = quantise(late[u + 1], "w4q%d" % (u + 1))
+            for e in range(2):
+                add_skip(toned_pair[:, e * PICK:(e + 1) * PICK], 2 * u + e, 0, PICK, "summed_pair%d" % e)
+            scale_all(2 * u)
+            if u + 1 < NT // 2:
+                th = curve_pair(u + 1)
+            scale_all(2 * u + 1)
+            if u + 2 < NT // 2:
+                late[u + 2] = round_pair([w4_raw[0, 1], w4_raw[1, 1]], u, "hold%d" % (u + 4))
+            put(2 * u)
+            store(2 * u)
+            if u + 1 < NT // 2:
+                toned_pair = tone(th[:], 2 * u + 2, 0, 2 * PICK, ("x_first", "x_planes0")[u % 2])
+            put(2 * u + 1)
+            store(2 * u + 1)

from contextlib import ExitStack

import concourse.mybir as mybir

K, H, T, S, PICK = 512, 1024, 4096, 1024, 512
FLOPS = 3 * 2 * K * H * S + 2 * H * H * PICK

F32 = mybir.dt.float32
BF16 = mybir.dt.bfloat16
I32 = mybir.dt.int32
U32 = mybir.dt.uint32
U16 = mybir.dt.uint16
U8 = mybir.dt.uint8
FP8X4 = mybir.dt.float8_e4m3fn_x4
FP4X4 = mybir.dt.float4_e2m1fn_x4
ALU = mybir.AluOpType
ACT = mybir.ActivationFunctionType

P = 128
PACK = 4
KP = P * PACK
NB = H // KP
NT = NB * PACK
BANK = 512
W3_ROW = 4


def tile_list_printhead_dot_features_kernel(
    tc, tab_words, tab_scales, offs, pos1, w1, w2_words, w2_scales, w3_words, w3_scales, gain, w4, ribbon, skip, wgo, out
):
    nc = tc.nc
    with ExitStack() as ctx:
        lists = ctx.enter_context(tc.tile_pool(name="lists", bufs=1))
        keep = ctx.enter_context(tc.tile_pool(name="keep", bufs=1))
        ring = ctx.enter_context(tc.tile_pool(name="ring", bufs=3))
        psum = ctx.enter_context(tc.psum_pool(name="psum", bufs=8))

        idx = lists.tile([P, S // 16], U16, name="idx")
        nc.sync.dma_start(idx[:], offs)
        p1 = lists.tile([P, PICK // 16], U16, name="p1")
        nc.sync.dma_start(p1[:], pos1)

        def load_weight(src_rows, b, stage, align=None):
            raw = keep.tile([P, PACK, KP], F32, name="raw", tag=stage, align_bytes=align)
            nc.sync.dma_start(raw[:], src_rows[:, b * KP:(b + 1) * KP].rearrange("(p j) c -> p j c", j=PACK))
            return raw

        def round_into(grouped, a, raw, pair):
            dst = grouped[:, a * 2 * KP:(a + 1) * 2 * KP].rearrange("p (t m j) -> p m t j", t=2, j=PACK)
            src = raw[:].rearrange("p j (m t) -> p m t j", t=PACK)
            src = src[:, :, 2 * pair:2 * pair + 2, :]
            nc.scalar.copy(out=dst, in_=src)

        def round_pair(raws, pair, tag):
            grouped = keep.tile([P, len(raws) * 2 * KP], BF16, name="grouped", tag=tag, align_bytes=64)
            for a, raw in enumerate(raws):
                round_into(grouped, a, raw, pair)
            return grouped

        def mx_tiles(name, width, tag=None):
            codes = keep.tile([P, width], U32, name=name + "_codes", tag=tag or name + "_codes", align_bytes=64)
            scales = keep.tile([P, width], U8, name=name + "_scales", align_bytes=64)
            return codes, scales

        def quantise_cols(tiles, grouped, c0, c1):
            nc.vector.quantize_mx(out=tiles[0][:, c0:c1].bitcast(FP8X4), scales=tiles[1][:, c0:c1], in_=grouped[:])

        def quantise(grouped, name, tag=None):
            width = grouped.shape[1] // PACK
            tiles = mx_tiles(name, width, tag)
            quantise_cols(tiles, grouped, 0, width)
            return tiles

        gain_sb = keep.tile([P, NT], F32, name="gain_sb")
        nc.sync.dma_start(gain_sb[:].rearrange("p (b i) -> p b i", i=PACK), gain.rearrange("(b p i) -> p b i", b=NB, i=PACK))
        skip_sb = keep.tile([P, NT], F32, name="skip_sb")
        nc.sync.dma_start(skip_sb[:].rearrange("p (b i) -> p b i", i=PACK), skip.rearrange("(b p i) -> p b i", b=NB, i=PACK))
        w1_raw = load_weight(w1, 0, "stage_a")
        w2_dram = w2_words[0].bitcast(I32)
        w3_dram = w3_words[0].rearrange("p n t -> p (n t)").bitcast(I32)

        def load_packed(b):
            w2_raw = keep.tile([P, 2 * KP], U8, name="w2_raw", tag="stage_c")
            nc.sync.dma_start(w2_raw[:].bitcast(I32), w2_dram[:, b * KP // 2:(b + 1) * KP // 2])
            w3_raw = keep.tile([P, KP], U32, name="w3_raw", tag="stage_d")
            nc.sync.dma_start(w3_raw[:].bitcast(I32), w3_dram[:, b * KP:(b + 1) * KP])
            return w2_raw, w3_raw

        w23_raw = load_packed(0)
        gs = keep.tile([P, NT], F32, name="gs")
        nc.vector.tensor_tensor(gs[:], gain_sb[:], skip_sb[:], ALU.mult)
        tab_w = keep.tile([P, T], U32, name="tab_w", tag="big")
        nc.sync.dma_start(tab_w[:].bitcast(I32), tab_words[0].rearrange("p n t -> p (n t)").bitcast(I32))
        tab_s = keep.tile([P, T], U8, name="tab_s", tag="stage_b")
        nc.vector.memset(tab_s[:].bitcast(I32), 0)
        for q in range(4):
            nc.scalar.dma_start(tab_s[32 * q:32 * q + 4, :].bitcast(I32), tab_scales[0, 4 * q:4 * q + 4, :].bitcast(I32))
        ws_raw = keep.tile([P, H], U8, name="ws_raw", tag="ws_raw")
        nc.gpsimd.memset(ws_raw[:].bitcast(I32), 0)
        for q in range(4):
            r0 = 32 * q + W3_ROW
            nc.gpsimd.dma_start(ws_raw[r0:r0 + 4, :].bitcast(I32), w3_scales[0, 4 * q:4 * q + 4, :].bitcast(I32))
        for q in range(4):
            queue = nc.gpsimd if q == 0 else nc.sync
            queue.dma_start(ws_raw[32 * q:32 * q + 4, :].bitcast(I32), w2_scales[0, 4 * q:4 * q + 4, :].bitcast(I32))

        w1_grouped = [round_pair([w1_raw], u, "w1_grouped%d" % u) for u in range(2)]
        v_s = keep.tile([P, S], U8, name="v_s", align_bytes=64)
        nc.vector.tensor_copy(v_s[:], tab_s[:].indirect(idx[:]))
        w1q = {u: quantise(w1_grouped[u], "w1q%d" % u) for u in range(2)}
        v_w = []
        for hf in range(S // BANK):
            vw = keep.tile([P, BANK], U32, name="v_w%d" % hf, align_bytes=64)
            cols = BANK // 16
            nc.vector.tensor_copy(vw[:], tab_w[:].indirect(idx[:, hf * cols:(hf + 1) * cols]))
            v_w.append(vw)

        def deal_packed(b, w2_raw, w3_raw):
            w3c = keep.tile([P, KP], U32, name="w3c%d" % b, align_bytes=64)
            nc.scalar.copy(out=w3c[:].rearrange("p (i m) -> p m i", i=PACK), in_=w3_raw[:].rearrange("p (m i) -> p m i", i=PACK))
            w2c = keep.tile([P, 2 * KP], U8, name="w2c%d" % b, align_bytes=64)
            nc.scalar.copy(
                out=w2c[:].bitcast(U16).rearrange("p (i m) -> p m i", i=PACK),
                in_=w2_raw[:].bitcast(U16).rearrange("p (m i) -> p m i", i=PACK),
            )
            wsc = keep.tile([P, KP], U8, name="wsc%d" % b, align_bytes=64)
            nc.vector.tensor_copy(
                out=wsc[:].rearrange("p (i m) -> p m i", i=PACK),
                in_=ws_raw[:, b * KP:(b + 1) * KP].rearrange("p (m i) -> p m i", i=PACK),
            )
            return w2c, w3c, wsc

        packed = {0: deal_packed(0, *w23_raw)}

        w1_raw = load_weight(w1, 1, "stage_a")
        w23_raw = load_packed(1)
        w4_raw = {(0, 0): load_weight(w4[0:KP, :], 0, "stage_b"), (1, 0): load_weight(w4[KP:2 * KP, :], 0, "big")}

        best = [keep.tile([P, S], F32, name="best%d" % t, tag="best%d" % t, align_bytes=64) for t in range(NT)]
        picked = [keep.tile([P, PICK], F32, name="picked%d" % t) for t in range(NT)]
        halves = ((0, PICK // 2), (PICK // 2, PICK))
        x_first = keep.tile([P, PICK * PACK], BF16, name="x_first", tag="x_first", align_bytes=64)
        x_last = {c0: keep.tile([P, (c1 - c0) * PACK], BF16, name="x_last%d" % c0, tag="x_last%d" % c0, align_bytes=64) for c0, c1 in halves}
        x_planes = [keep.tile([P, PACK, PICK], BF16, name="x_planes%d" % b, tag="x_planes%d" % b, align_bytes=64) for b in range(NB)]
        xq = {}
        w4q = {}

        ones = {}

        def product(bank, lhsT, lhsT_scale, hf):
            nc.tensor.matmul_mx(out=bank[:], lhsT=lhsT, lhsT_scale=lhsT_scale, rhs=v_w[hf][:].bitcast(FP8X4),
                                rhs_scale=v_s[:, hf * BANK:(hf + 1) * BANK], start=True, stop=True)

        def lead(t):
            w1c, w1s = w1q[t // 2]
            cols = slice((t % 2) * P, (t % 2 + 1) * P)
            for hf in range(S // BANK):
                bank = psum.tile([P, BANK], F32, name="lead_bank", tag="lead_bank", bufs=2)
                product(bank, w1c[:, cols].bitcast(FP8X4), w1s[:, cols], hf)
                ones[t, hf] = ring.tile([P, BANK], F32, name="one", tag="one", bufs=8)
                nc.scalar.copy(out=ones[t, hf][:], in_=bank[:])

        def first_stage(t):
            b, i = divmod(t, PACK)
            cols = slice(i * P, (i + 1) * P)
            w2c, w3c, wsc = packed[b]
            held = []
            for hf in range(S // BANK):
                banks = [psum.tile([P, BANK], F32, name="bank", tag="bank", bufs=6) for n in range(2)]
                product(banks[0], w2c[:, 2 * i * P:2 * (i + 1) * P].bitcast(FP4X4), wsc[:, cols], hf)
                product(banks[1], w3c[:, cols].bitcast(FP8X4), wsc[W3_ROW:P, cols], hf)
                two = ring.tile([P, BANK], F32, name="two", tag="two")
                nc.vector.tensor_tensor(two[:], ones[t, hf][:], banks[0][:], ALU.max)
                held.append((banks[1], two))
            for hf in range(S // BANK):
                nc.vector.tensor_tensor(best[t][:, hf * BANK:(hf + 1) * BANK], held[hf][1][:], held[hf][0][:], ALU.max)

        def pick(t, c0=0, c1=PICK):
            nc.vector.tensor_copy(picked[t][:, c0:c1], best[t][:].indirect(p1[:, c0 // 16:c1 // 16]))

        def round_picked(t, c0=0, c1=PICK):
            b, i = divmod(t, PACK)
            if t < NT - 1:
                dst = x_planes[b][:, i, c0:c1]
            else:
                dst = x_last[c0][:].rearrange("p (m i) -> p i m", i=PACK)[:, i, :]
            nc.scalar.activation(out=dst, in_=picked[t][:, c0:c1], func=ACT.Copy, scale=gain_sb[:, t:t + 1])

        def weave(dst, b, planes, c0, c1):
            src = x_planes[b][:, 0:planes, c0:c1].rearrange("p i (c e) -> p c i e", e=4)
            nc.scalar.copy(out=dst.rearrange("p (c e i) -> p c i e", e=4, i=PACK)[:, :, 0:planes, :], in_=src)

        out_rows = out.rearrange("(b p i) j -> b i p j", b=NB, i=PACK)
        result, toned, summed = {}, {}, {}
        result_tags = ["x_last256", "hold2", "hold3"] + ["best%d" % (t - 2) for t in range(3, NT)]

        def scale_all(t):
            result[t] = keep.tile([P, S], F32, name="result", tag=result_tags[t], align_bytes=64)
            nc.scalar.activation(out=result[t][:], in_=best[t][:], func=ACT.Copy, scale=gs[:, t:t + 1])

        for t in range(PACK):
            lead(t)
        packed[1] = deal_packed(1, *w23_raw)
        for u in range(2):
            w1q[2 + u] = quantise(round_pair([w1_raw], u, "w1_grouped%d" % u), "w1q%d" % (2 + u))
        ribbon_rows = ribbon.rearrange("(b p i) m -> b p (i m)", b=NB, i=PACK)
        ribbon_sb = []
        for b, stage in enumerate(("stage_c", "ws_raw")):
            part = keep.tile([P, PACK * PICK], F32, name="ribbon_sb", tag=stage)
            nc.sync.dma_start(part[:], ribbon_rows[b])
            ribbon_sb.append(part)
        wgo_sb = keep.tile([P, PACK, PICK], F32, name="wgo_sb", tag="stage_d")
        for q in range(4):
            nc.sync.dma_start(wgo_sb[32 * q:32 * q + 32].rearrange("p i m -> p (i m)"), wgo.rearrange("(p i) m -> p (i m)", i=PACK))
        w4_raw[0, 1] = load_weight(w4[0:KP, :], 1, "stage_a")
        w4_raw[1, 1] = load_weight(w4[KP:2 * KP, :], 1, "w1_grouped1", 64)
        w4_grouped = [keep.tile([P, 4 * KP], BF16, name="w4_grouped%d" % u, tag="w4_grouped%d" % u, align_bytes=64) for u in range(2)]
        for t in range(NT):
            first_stage(t)
            if t < PACK:
                lead(t + PACK)
            if 0 < t < NT - 1:
                pick(t - 1)
            if t == NT - 2:
                pick(t)
        for u in range(2):
            for a in range(NB):
                round_into(w4_grouped[u], a, w4_raw[a, 0], u)
        for t in range(PACK):
            round_picked(t)
        for c0 in range(0, PICK, P):
            weave(x_first[:, PACK * c0:PACK * (c0 + P)], 0, PACK, c0, c0 + P)
        xq[0] = quantise(x_first, "xq0")
        for t in range(PACK, NT - 1):
            round_picked(t)
        for c0, c1 in halves:
            weave(x_last[c0][:], 1, PACK - 1, c0, c1)
        xq[1] = mx_tiles("xq1", PICK)
        for c0, c1 in halves:
            pick(NT - 1, c0, c1)
            round_picked(NT - 1, c0, c1)
        w4q[0] = quantise(w4_grouped[0], "w4q0", "x_planes1")
        for c0, c1 in halves:
            quantise_cols(xq[1], x_last[c0], c0, c1)
        w4q[1] = quantise(w4_grouped[1], "w4q1", "x_last0")
        scale_all(0)

        def second_stage(th, t, c0=0, c1=PICK):
            bank = psum.tile([P, c1 - c0], F32, name="bank", tag="bank", bufs=6)
            wc, wsc = w4q[t // 2]
            for a in range(NB):
                cols = slice((2 * a + t % 2) * P, (2 * a + t % 2 + 1) * P)
                xc, xs = xq[a]
                nc.tensor.matmul_mx(out=bank[:], lhsT=wc[:, cols].bitcast(FP8X4), lhsT_scale=wsc[:, cols],
                                    rhs=xc[:, c0:c1].bitcast(FP8X4), rhs_scale=xs[:, c0:c1], start=(a == 0), stop=(a == NB - 1))
            nc.scalar.activation(out=th, in_=bank[:], func=ACT.Tanh)

        def tone(th, t, c0, width, tag):
            tile = keep.tile([P, width], F32, name="toned", tag=tag, align_bytes=64)
            first = (t % PACK) * PICK + c0
            nc.vector.tensor_tensor(tile[:], th, ribbon_sb[t // PACK][:, first:first + width], ALU.mult)
            return tile

        def add_skip(toned_part, t, c0, c1, tag):
            summed[t, c0] = keep.tile([P, c1 - c0], F32, name="summed", tag=tag, align_bytes=64)
            nc.vector.scalar_tensor_tensor(summed[t, c0][:], picked[t][:, c0:c1], gs[:, t:t + 1], toned_part, ALU.mult, ALU.add)

        def put(t, c0=0, c1=PICK):
            nc.vector.tensor_tensor(result[t][:].indirect(p1[:, c0 // 16:c1 // 16]), summed[t, c0][:], wgo_sb[:, t % PACK, c0:c1], ALU.mult)

        def store(t):
            b, i = divmod(t, PACK)
            nc.sync.dma_start(out_rows[b, i], result[t][:])

        def curve_pair(u):
            th = keep.tile([P, 2 * PICK], F32, name="th_pair", tag="w4_grouped%d" % ((u - 1) % 2), align_bytes=64)
            for e in range(2):
                second_stage(th[:, e * PICK:(e + 1) * PICK], 2 * u + e)
            return th

        half_th, half_toned = [], []
        for n, (c0, c1) in enumerate(halves):
            th = keep.tile([P, c1 - c0], F32, name="th", tag="hold%d" % n, align_bytes=64)
            second_stage(th[:], 0, c0, c1)
            half_th.append(th)
        th1 = ring.tile([P, PICK], F32, name="th1", tag="two")
        second_stage(th1[:], 1)
        for n, (c0, c1) in enumerate(halves):
            half_toned.append(tone(half_th[n][:], 0, c0, c1 - c0, "hold%d" % (2 + n)))
        for n, (c0, c1) in enumerate(halves):
            add_skip(half_toned[n][:], 0, c0, c1, "hold%d" % (4 + n))
        put(0, *halves[0])
        toned1 = tone(th1[:], 1, 0, PICK, "toned1")
        put(0, *halves[1])
        store(0)
        add_skip(toned1[:], 1, 0, PICK, "summed1")
        th = curve_pair(1)
        scale_all(1)
        late = {u: round_pair([w4_raw[0, 1], w4_raw[1, 1]], u - 2, "hold%d" % (u + 2)) for u in (2,)}
        toned_pair = tone(th[:], 2, 0, 2 * PICK, "x_first")
        put(1)
        store(1)
        for u in range(1, NT // 2):
            if u + 1 < NT // 2:
                w4q[u + 1] = quantise(late[u + 1], "w4q%d" % (u + 1))
            for e in range(2):
                add_skip(toned_pair[:, e * PICK:(e + 1) * PICK], 2 * u + e, 0, PICK, "summed_pair%d" % e)
            scale_all(2 * u)
            if u + 1 < NT // 2:
                th = curve_pair(u + 1)
            scale_all(2 * u + 1)
            if u + 2 < NT // 2:
                late[u + 2] = round_pair([w4_raw[0, 1], w4_raw[1, 1]], u, "hold%d" % (u + 4))
            put(2 * u)
            store(2 * u)
            if u + 1 < NT // 2:
                toned_pair = tone(th[:], 2 * u + 2, 0, 2 * PICK, ("x_first", "x_planes0")[u % 2])
            put(2 * u + 1)
            store(2 * u + 1)
